import numpy as np, ml_dtypes
CORES = [45,53,77,117,47,55,79,119]
N = 8
F = 128
GROUPS = [[0,2,4,6],[1,3,5,7]]
def setup_inputs(rng):
    return {"x": rng.standard_normal((N, 128, F), dtype=np.float32).astype(ml_dtypes.bfloat16), "w": (rng.standard_normal((N, 128, 128), dtype=np.float32) / 11).astype(ml_dtypes.bfloat16)}
def setup_inputs_big(rng):
    d = setup_inputs(rng)
    for k in ("x", "w"): d[k] = (d[k].astype(np.float32) * 1024.0).astype(d[k].dtype)
    return d
def setup_inputs_small(rng):
    d = setup_inputs(rng)
    for k in ("x", "w"): d[k] = (d[k].astype(np.float32) * (1 / 1024.0)).astype(d[k].dtype)
    return d
def setup_inputs_apart(rng):
    d = setup_inputs(rng)
    f = (10.0 ** rng.permutation(np.linspace(-1.5, 1.5, N))).astype(np.float32).reshape(N, 1, 1)
    for k in ("x", "w"): d[k] = (d[k].astype(np.float32) * f).astype(d[k].dtype)
    return d
def reference(x, w):
    X, W = x.astype(np.float64), w.astype(np.float64)
    s = sum(W[g[0]].T @ np.maximum(sum(X[j] for j in g), 0.0) for g in GROUPS).astype(ml_dtypes.bfloat16)
    return {"y": np.broadcast_to(s, (N,) + s.shape)}

@@ -1,0 +1,155 @@
+from concourse.bass import DstId, RemoteDMATransfer
+from concourse.mybir import AluOpType
+
+F = 128
+M = 4
+NG = 2
+
+SCRATCH = {
+    "xs": ("sbuf", [128, F], "bfloat16"),
+    "ws": ("sbuf", [128, 128], "bfloat16"),
+    "xl": ("sbuf", [128, M * F], "bfloat16"),
+    "zero": ("sbuf", [128, F], "bfloat16"),
+    "ts": ("sbuf", [128, F], "bfloat16"),
+    "pl": ("sbuf", [128, NG * F], "bfloat16"),
+    "ys": ("sbuf", [128, F], "bfloat16"),
+    "acc": ("psum", [128, 512], "float32"),
+    "pp": ("psum", [128, 512], "float32"),
+}
+SEMAPHORES = ["ldx", "ldw", "zf", "ax0", "ax1", "ax2", "ax3", "aw", "vs", "tr", "mm", "pr", "ap", "yr", "st", "snt"]
+
+
+def _bits(mask):
+    return [b for b in range(mask.bit_length()) if (mask >> b) & 1]
+
+
+def _mk(bits):
+    m = 0
+    for b in bits:
+        m |= 1 << b
+    return m
+
+
+def _plan(T, topo):
+    cores = list(T.cores)
+    groups = [[cores[r] for r in grp] for grp in T.tables["GROUPS"]]
+    chips, lead = [], []
+    for mem in groups:
+        out = [c for c in cores if c not in mem]
+        ch = sorted(set(topo.chip(c) for c in mem))
+        chips.append(ch)
+        lead.append([[c for c in mem if topo.chip(c) == h and all(topo.may_write(c, d) for d in out)][0] for h in ch])
+    hop1, hop2 = {}, {}
+    for gi, mem in enumerate(groups):
+        for k, c in enumerate(mem):
+            to = sorted([l for l in lead[gi] if l != c], key=lambda l: topo.chip(l) == topo.chip(c))
+            hop1[c] = [("x", k, to)] + ([("w", 0, to)] if k == 0 else [])
+            hop2[c] = []
+        for i, l in enumerate(lead[gi]):
+            to = []
+            for gj, mem2 in enumerate(groups):
+                if gj != gi:
+                    assert len(chips[gj]) == len(lead[gi])
+                    to += sorted([c for c in mem2 if topo.chip(c) == chips[gj][i]], key=lambda c: c in lead[gj])
+            to += [c for c in mem if topo.chip(c) == topo.chip(l) and c != l]
+            hop2[l] = [("p", gi, to)]
+    calls = {}
+    for c in cores:
+        allowed = None
+        for _, _, to in hop1[c] + hop2[c]:
+            for d in to:
+                assert topo.may_write(c, d)
+                allowed = topo.mask(c, d) if allowed is None else allowed & topo.mask(c, d)
+        eng = _bits(allowed)
+        calls[c] = []
+        for hop in (hop1[c], hop2[c]):
+            n = len(eng) // max(1, len(hop))
+            calls[c].append([(kind, s, to, eng[i * n:(i + 1) * n]) for i, (kind, s, to) in enumerate(hop) if to])
+    return groups, lead, calls
+
+
+def _semname(kind, slot):
+    return {"x": "ax%d" % slot, "w": "aw", "p": "ap"}[kind]
+
+
+def rank_program(g, core, T, topo):
+    if T.rank_of(core) is None:
+        return
+    S = T.sem
+    groups, lead, calls = _plan(T, topo)
+    gi = [i for i, mem in enumerate(groups) if core in mem][0]
+    mem = groups[gi]
+    pos = mem.index(core)
+    leader = core in lead[gi]
+
+    def col(buf, k):
+        return buf[:, k * F:(k + 1) * F]
+
+    due, eta = {}, {}
+    for c, hops in calls.items():
+        for hop in hops:
+            for kind, s, to, eng in hop:
+                if core in to:
+                    nm = _semname(kind, s)
+                    due[nm] = due.get(nm, 0) + len(eng)
+                    eta[nm] = ((to.index(core) + 1) * 128 // len(eng), topo.chip(c) != topo.chip(core))
+
+    sent = [0]
+
+    def issue(hop):
+        trs = []
+        for kind, s, to, eng in hop:
+            src = {"x": T.xs[:], "w": T.ws[:], "p": col(T.pl, s)}[kind]
+            dst = {"x": col(T.xl, s), "w": T.ws[:], "p": col(T.pl, s)}[kind]
+            ids = [DstId(rid=topo.addr(d)[0], pnc=topo.addr(d)[1]) for d in to]
+            trs.append(RemoteDMATransfer(dst_ids=ids, dma_engine_mask=_mk(eng), remote_sem=S[_semname(kind, s)],
+                                         srcs=[src], dsts=[dst for _ in to], alu_op=0))
+            sent[0] += len(eng)
+        if trs:
+            g.remote_dma_fused(trs, local_sem=S.snt)
+
+    g.sync.dma_start(T.xs[:], T.x[:]).then_inc(S.ldx, 16)
+    if pos == 0:
+        g.scalar.dma_start(T.ws[:], T.w[:]).then_inc(S.ldw, 16)
+
+    g.wait_ge(S.ldx, 16)
+    if pos == 0:
+        g.wait_ge(S.ldw, 16)
+    issue(calls[core][0])
+
+    v = g.vector
+    own = T.pp[:, 0:F]
+    if leader:
+        v.memset(T.zero[:], 0.0).then_inc(S.zf, 1)
+        v.wait_ge(S.ldx, 16)
+        run, n = T.xs[:], 0
+        for nm in sorted([a for a in due if a.startswith("ax")], key=lambda a: eta[a]):
+            v.wait_ge(S[nm], due[nm])
+            if n:
+                v.wait_ge(S.vs, n)
+            nxt = col(T.acc, n)
+            v.tensor_tensor(nxt, run, col(T.xl, int(nm[2:])), AluOpType.add).then_inc(S.vs, 1)
+            run, n = nxt, n + 1
+        v.wait_ge(S.vs, n)
+        v.wait_ge(S.zf, 1)
+        v.tensor_tensor(T.ts[:], run, T.zero[:], AluOpType.max).then_inc(S.tr, 1)
+        g.tensor.wait_ge(S.tr, 1)
+        if pos == 0:
+            g.tensor.wait_ge(S.ldw, 16)
+        else:
+            g.tensor.wait_ge(S.aw, due["aw"])
+        g.tensor.matmul(own, T.ws[:], T.ts[:], start=True, stop=True).then_inc(S.mm, 1)
+        v.wait_ge(S.mm, 1)
+        v.tensor_copy(col(T.pl, gi), own).then_inc(S.pr, 1)
+        g.wait_ge(S.pr, 1)
+        issue(calls[core][1])
+        v.wait_ge(S.ap, due["ap"])
+        v.tensor_tensor(T.ys[:], own, col(T.pl, 1 - gi), AluOpType.add).then_inc(S.yr, 1)
+    else:
+        v.wait_ge(S.ap, due["ap"])
+        v.tensor_tensor(T.ys[:], col(T.pl, 0), col(T.pl, 1), AluOpType.add).then_inc(S.yr, 1)
+
+    g.sync.wait_ge(S.yr, 1)
+    g.sync.dma_start(T.y[:], T.ys[:]).then_inc(S.st, 16)
+    g.wait_ge(S.snt, sent[0])
+    g.wait_ge(S.st, 16)

@@ -2,6 +2,7 @@ from concourse.bass import DstId, RemoteDMATransfer
 from concourse.mybir import AluOpType
 
 F = 128
+H = F // 2
 M = 4
 NG = 2
 
@@ -9,14 +10,20 @@ SCRATCH = {
     "xs": ("sbuf", [128, F], "bfloat16"),
     "ws": ("sbuf", [128, 128], "bfloat16"),
     "xl": ("sbuf", [128, M * F], "bfloat16"),
-    "zero": ("sbuf", [128, F], "bfloat16"),
+    "zero": ("sbuf", [128, H], "bfloat16"),
+    "zi": ("sbuf", [128, 129], "bfloat16"),
+    "idd": ("dram", [129, 128], "bfloat16"),
+    "idn": ("sbuf", [128, 128], "bfloat16"),
     "ts": ("sbuf", [128, F], "bfloat16"),
     "pl": ("sbuf", [128, NG * F], "bfloat16"),
     "ys": ("sbuf", [128, F], "bfloat16"),
-    "acc": ("psum", [128, 512], "float32"),
-    "pp": ("psum", [128, 512], "float32"),
+    "acc0": ("psum", [128, 512], "float32"),
+    "acc1": ("psum", [128, 512], "float32"),
+    "pp0": ("psum", [128, 512], "float32"),
+    "pp1": ("psum", [128, 512], "float32"),
 }
-SEMAPHORES = ["ldx", "ldw", "zf", "ax0", "ax1", "ax2", "ax3", "aw", "vs", "tr", "mm", "pr", "ap", "yr", "st", "snt"]
+SEMAPHORES = ["ldx", "ldw", "zf", "ax0", "ax1", "ax2", "ax3", "aw", "zi1", "id1", "id2", "sm0", "sm1", "tr0", "tr1",
+              "mm0", "mm1", "pr", "ap", "yr", "st", "snt"]
 
 
 def _bits(mask):
@@ -30,6 +37,11 @@ def _mk(bits):
     return m
 
 
+def _share(trs, eng):
+    n = len(eng) // max(1, len(trs))
+    return [(k, s, to, eng[i * n:(i + 1) * n]) for i, (k, s, to) in enumerate(trs)]
+
+
 def _plan(T, topo):
     cores = list(T.cores)
     groups = [[cores[r] for r in grp] for grp in T.tables["GROUPS"]]
@@ -39,32 +51,36 @@ def _plan(T, topo):
         ch = sorted(set(topo.chip(c) for c in mem))
         chips.append(ch)
         lead.append([[c for c in mem if topo.chip(c) == h and all(topo.may_write(c, d) for d in out)][0] for h in ch])
-    hop1, hop2 = {}, {}
+    calls = {}
     for gi, mem in enumerate(groups):
         for k, c in enumerate(mem):
-            to = sorted([l for l in lead[gi] if l != c], key=lambda l: topo.chip(l) == topo.chip(c))
-            hop1[c] = [("x", k, to)] + ([("w", 0, to)] if k == 0 else [])
-            hop2[c] = []
-        for i, l in enumerate(lead[gi]):
-            to = []
-            for gj, mem2 in enumerate(groups):
-                if gj != gi:
-                    assert len(chips[gj]) == len(lead[gi])
-                    to += sorted([c for c in mem2 if topo.chip(c) == chips[gj][i]], key=lambda c: c in lead[gj])
-            to += [c for c in mem if topo.chip(c) == topo.chip(l) and c != l]
-            hop2[l] = [("p", gi, to)]
-    calls = {}
-    for c in cores:
-        allowed = None
-        for _, _, to in hop1[c] + hop2[c]:
-            for d in to:
-                assert topo.may_write(c, d)
-                allowed = topo.mask(c, d) if allowed is None else allowed & topo.mask(c, d)
-        eng = _bits(allowed)
-        calls[c] = []
-        for hop in (hop1[c], hop2[c]):
-            n = len(eng) // max(1, len(hop))
-            calls[c].append([(kind, s, to, eng[i * n:(i + 1) * n]) for i, (kind, s, to) in enumerate(hop) if to])
+            far = [l for l in lead[gi] if topo.chip(l) != topo.chip(c)]
+            near = [l for l in lead[gi] if topo.chip(l) == topo.chip(c) and l != c]
+            cross, home = [], []
+            if c in lead[gi]:
+                i = lead[gi].index(c)
+                for gj, mem2 in enumerate(groups):
+                    if gj != gi:
+                        assert len(chips[gj]) == len(lead[gi])
+                        cross += sorted([d for d in mem2 if topo.chip(d) == chips[gj][i]], key=lambda d: d in lead[gj])
+                home = [d for d in mem if topo.chip(d) == topo.chip(c) and d != c]
+            out_mask, in_mask = None, 0
+            for d in far + cross:
+                out_mask = topo.mask(c, d) if out_mask is None else out_mask & topo.mask(c, d)
+            for d in near + home:
+                in_mask |= topo.mask(c, d)
+            e_far = _bits(out_mask)
+            e_near = _bits(in_mask & ~out_mask)
+            first = [("x", k, far)]
+            second_far = [("w", 0, far)] if k == 0 else []
+            second_near = ([("x", k, near)] + ([("w", 0, near)] if k == 0 else [])) if near else []
+            hop1 = [_share(first, e_far), _share(second_far, e_far) + _share(second_near, e_near)]
+            hop2 = [_share([("p", gi, cross)], e_far) if cross else [], _share([("p", gi, home)], e_near) if home else []]
+            calls[c] = [[x for x in hop1 if x], [x for x in hop2 if x]]
+            for hop in calls[c]:
+                for call in hop:
+                    for _, _, to, _ in call:
+                        assert all(topo.may_write(c, d) for d in to)
     return groups, lead, calls
 
 
@@ -85,71 +101,91 @@ def rank_program(g, core, T, topo):
     def col(buf, k):
         return buf[:, k * F:(k + 1) * F]
 
+    def half(buf, k, h):
+        return buf[:, k * F + h * H:k * F + (h + 1) * H]
+
     due, eta = {}, {}
     for c, hops in calls.items():
         for hop in hops:
-            for kind, s, to, eng in hop:
-                if core in to:
-                    nm = _semname(kind, s)
-                    due[nm] = due.get(nm, 0) + len(eng)
-                    eta[nm] = ((to.index(core) + 1) * 128 // len(eng), topo.chip(c) != topo.chip(core))
+            for ci, call in enumerate(hop):
+                for kind, s, to, eng in call:
+                    if core in to:
+                        nm = _semname(kind, s)
+                        due[nm] = due.get(nm, 0) + len(eng)
+                        eta[nm] = (ci, (to.index(core) + 1) * 128 // len(eng))
 
     sent = [0]
+    waited = []
 
     def issue(hop):
-        trs = []
-        for kind, s, to, eng in hop:
-            src = {"x": T.xs[:], "w": T.ws[:], "p": col(T.pl, s)}[kind]
-            dst = {"x": col(T.xl, s), "w": T.ws[:], "p": col(T.pl, s)}[kind]
-            ids = [DstId(rid=topo.addr(d)[0], pnc=topo.addr(d)[1]) for d in to]
-            trs.append(RemoteDMATransfer(dst_ids=ids, dma_engine_mask=_mk(eng), remote_sem=S[_semname(kind, s)],
-                                         srcs=[src], dsts=[dst for _ in to], alu_op=0))
-            sent[0] += len(eng)
-        if trs:
+        for call in hop:
+            trs = []
+            for kind, s, to, eng in call:
+                if kind not in waited:
+                    ready = {"x": (S.ldx, 16), "w": (S.ldw, 16), "p": (S.pr, 2)}[kind]
+                    g.wait_ge(ready[0], ready[1])
+                    waited.append(kind)
+                src = {"x": T.xs[:], "w": T.ws[:], "p": col(T.pl, s)}[kind]
+                dst = {"x": col(T.xl, s), "w": T.ws[:], "p": col(T.pl, s)}[kind]
+                ids = [DstId(rid=topo.addr(d)[0], pnc=topo.addr(d)[1]) for d in to]
+                trs.append(RemoteDMATransfer(dst_ids=ids, dma_engine_mask=_mk(eng), remote_sem=S[_semname(kind, s)],
+                                             srcs=[src], dsts=[dst for _ in to], alu_op=0))
+                sent[0] += len(eng)
             g.remote_dma_fused(trs, local_sem=S.snt)
 
     g.sync.dma_start(T.xs[:], T.x[:]).then_inc(S.ldx, 16)
     if pos == 0:
         g.scalar.dma_start(T.ws[:], T.w[:]).then_inc(S.ldw, 16)
 
-    g.wait_ge(S.ldx, 16)
-    if pos == 0:
-        g.wait_ge(S.ldw, 16)
     issue(calls[core][0])
 
     v = g.vector
-    own = T.pp[:, 0:F]
+    pe = g.tensor
     if leader:
+        acc = [T.acc0[:, 0:H], T.acc1[:, 0:H]]
+        own = [T.pp0[:, 0:H], T.pp1[:, 0:H]]
+        v.memset(T.zi[:, 0:1], 1.0).then_inc(S.zi1, 1)
+        v.memset(T.zi[:, 1:129], 0.0).then_inc(S.zi1, 1)
         v.memset(T.zero[:], 0.0).then_inc(S.zf, 1)
-        v.wait_ge(S.ldx, 16)
-        run, n = T.xs[:], 0
-        for nm in sorted([a for a in due if a.startswith("ax")], key=lambda a: eta[a]):
-            v.wait_ge(S[nm], due[nm])
-            if n:
-                v.wait_ge(S.vs, n)
-            nxt = col(T.acc, n)
-            v.tensor_tensor(nxt, run, col(T.xl, int(nm[2:])), AluOpType.add).then_inc(S.vs, 1)
-            run, n = nxt, n + 1
-        v.wait_ge(S.vs, n)
+        g.scalar.wait_ge(S.zi1, 2)
+        g.scalar.dma_start(T.idd[:], T.zi[:]).then_inc(S.id1, 16)
+        g.scalar.wait_ge(S.id1, 16)
+        g.scalar.dma_start(T.idn[:], T.idd[0:128, :]).then_inc(S.id2, 16)
+        pe.wait_ge(S.id2, 16)
+        pe.wait_ge(S.ldx, 16)
+        for h in range(2):
+            pe.matmul(acc[h], T.idn[:], half(T.xs, 0, h), start=True, stop=False)
+        order = sorted([a for a in due if a.startswith("ax")], key=lambda a: eta[a])
+        for nm in order:
+            pe.wait_ge(S[nm], due[nm])
+            for h in range(2):
+                last = nm == order[-1]
+                ins = pe.matmul(acc[h], T.idn[:], half(T.xl, int(nm[2:]), h), start=False, stop=last)
+                if last:
+                    ins.then_inc(S["sm%d" % h], 1)
         v.wait_ge(S.zf, 1)
-        v.tensor_tensor(T.ts[:], run, T.zero[:], AluOpType.max).then_inc(S.tr, 1)
-        g.tensor.wait_ge(S.tr, 1)
+        for h in range(2):
+            v.wait_ge(S["sm%d" % h], 1)
+            v.tensor_tensor(half(T.ts, 0, h), acc[h], T.zero[:], AluOpType.max).then_inc(S["tr%d" % h], 1)
         if pos == 0:
-            g.tensor.wait_ge(S.ldw, 16)
+            pe.wait_ge(S.ldw, 16)
         else:
-            g.tensor.wait_ge(S.aw, due["aw"])
-        g.tensor.matmul(own, T.ws[:], T.ts[:], start=True, stop=True).then_inc(S.mm, 1)
-        v.wait_ge(S.mm, 1)
-        v.tensor_copy(col(T.pl, gi), own).then_inc(S.pr, 1)
-        g.wait_ge(S.pr, 1)
+            pe.wait_ge(S.aw, due["aw"])
+        for h in range(2):
+            pe.wait_ge(S["tr%d" % h], 1)
+            pe.matmul(own[h], T.ws[:], half(T.ts, 0, h), start=True, stop=True).then_inc(S["mm%d" % h], 1)
+        for h in range(2):
+            v.wait_ge(S["mm%d" % h], 1)
+            v.tensor_copy(half(T.pl, gi, h), own[h]).then_inc(S.pr, 1)
         issue(calls[core][1])
         v.wait_ge(S.ap, due["ap"])
-        v.tensor_tensor(T.ys[:], own, col(T.pl, 1 - gi), AluOpType.add).then_inc(S.yr, 1)
+        for h in range(2):
+            v.tensor_tensor(half(T.ys, 0, h), own[h], half(T.pl, 1 - gi, h), AluOpType.add).then_inc(S.yr, 1)
     else:
         v.wait_ge(S.ap, due["ap"])
-        v.tensor_tensor(T.ys[:], col(T.pl, 0), col(T.pl, 1), AluOpType.add).then_inc(S.yr, 1)
+        v.tensor_tensor(T.ys[:], col(T.pl, 0), col(T.pl, 1), AluOpType.add).then_inc(S.yr, 2)
 
-    g.sync.wait_ge(S.yr, 1)
+    g.sync.wait_ge(S.yr, 2)
     g.sync.dma_start(T.y[:], T.ys[:]).then_inc(S.st, 16)
     g.wait_ge(S.snt, sent[0])
     g.wait_ge(S.st, 16)

from concourse.bass import DstId, RemoteDMATransfer
from concourse.mybir import AluOpType

F = 128
H = F // 2
M = 4
NG = 2

SCRATCH = {
    "xs": ("sbuf", [128, F], "bfloat16"),
    "ws": ("sbuf", [128, 128], "bfloat16"),
    "xl": ("sbuf", [128, M * F], "bfloat16"),
    "zero": ("sbuf", [128, H], "bfloat16"),
    "zi": ("sbuf", [128, 129], "bfloat16"),
    "idd": ("dram", [129, 128], "bfloat16"),
    "idn": ("sbuf", [128, 128], "bfloat16"),
    "ts": ("sbuf", [128, F], "bfloat16"),
    "pl": ("sbuf", [128, NG * F], "bfloat16"),
    "ys": ("sbuf", [128, F], "bfloat16"),
    "acc0": ("psum", [128, 512], "float32"),
    "acc1": ("psum", [128, 512], "float32"),
    "pp0": ("psum", [128, 512], "float32"),
    "pp1": ("psum", [128, 512], "float32"),
}
SEMAPHORES = ["ldx", "ldw", "zf", "ax0", "ax1", "ax2", "ax3", "aw", "zi1", "id1", "id2", "sm0", "sm1", "tr0", "tr1",
              "mm0", "mm1", "pr", "ap", "yr", "st", "snt"]


def _bits(mask):
    return [b for b in range(mask.bit_length()) if (mask >> b) & 1]


def _mk(bits):
    m = 0
    for b in bits:
        m |= 1 << b
    return m


def _share(trs, eng):
    n = len(eng) // max(1, len(trs))
    return [(k, s, to, eng[i * n:(i + 1) * n]) for i, (k, s, to) in enumerate(trs)]


def _plan(T, topo):
    cores = list(T.cores)
    groups = [[cores[r] for r in grp] for grp in T.tables["GROUPS"]]
    chips, lead = [], []
    for mem in groups:
        out = [c for c in cores if c not in mem]
        ch = sorted(set(topo.chip(c) for c in mem))
        chips.append(ch)
        lead.append([[c for c in mem if topo.chip(c) == h and all(topo.may_write(c, d) for d in out)][0] for h in ch])
    calls = {}
    for gi, mem in enumerate(groups):
        for k, c in enumerate(mem):
            far = [l for l in lead[gi] if topo.chip(l) != topo.chip(c)]
            near = [l for l in lead[gi] if topo.chip(l) == topo.chip(c) and l != c]
            cross, home = [], []
            if c in lead[gi]:
                i = lead[gi].index(c)
                for gj, mem2 in enumerate(groups):
                    if gj != gi:
                        assert len(chips[gj]) == len(lead[gi])
                        cross += sorted([d for d in mem2 if topo.chip(d) == chips[gj][i]], key=lambda d: d in lead[gj])
                home = [d for d in mem if topo.chip(d) == topo.chip(c) and d != c]
            out_mask, in_mask = None, 0
            for d in far + cross:
                out_mask = topo.mask(c, d) if out_mask is None else out_mask & topo.mask(c, d)
            for d in near + home:
                in_mask |= topo.mask(c, d)
            e_far = _bits(out_mask)
            e_near = _bits(in_mask & ~out_mask)
            first = [("x", k, far)]
            second_far = [("w", 0, far)] if k == 0 else []
            second_near = ([("x", k, near)] + ([("w", 0, near)] if k == 0 else [])) if near else []
            hop1 = [_share(first, e_far), _share(second_far, e_far) + _share(second_near, e_near)]
            hop2 = [_share([("p", gi, cross)], e_far) if cross else [], _share([("p", gi, home)], e_near) if home else []]
            calls[c] = [[x for x in hop1 if x], [x for x in hop2 if x]]
            for hop in calls[c]:
                for call in hop:
                    for _, _, to, _ in call:
                        assert all(topo.may_write(c, d) for d in to)
    return groups, lead, calls


def _semname(kind, slot):
    return {"x": "ax%d" % slot, "w": "aw", "p": "ap"}[kind]


def rank_program(g, core, T, topo):
    if T.rank_of(core) is None:
        return
    S = T.sem
    groups, lead, calls = _plan(T, topo)
    gi = [i for i, mem in enumerate(groups) if core in mem][0]
    mem = groups[gi]
    pos = mem.index(core)
    leader = core in lead[gi]

    def col(buf, k):
        return buf[:, k * F:(k + 1) * F]

    def half(buf, k, h):
        return buf[:, k * F + h * H:k * F + (h + 1) * H]

    due, eta = {}, {}
    for c, hops in calls.items():
        for hop in hops:
            for ci, call in enumerate(hop):
                for kind, s, to, eng in call:
                    if core in to:
                        nm = _semname(kind, s)
                        due[nm] = due.get(nm, 0) + len(eng)
                        eta[nm] = (ci, (to.index(core) + 1) * 128 // len(eng))

    sent = [0]
    waited = []

    def issue(hop):
        for call in hop:
            trs = []
            for kind, s, to, eng in call:
                if kind not in waited:
                    ready = {"x": (S.ldx, 16), "w": (S.ldw, 16), "p": (S.pr, 2)}[kind]
                    g.wait_ge(ready[0], ready[1])
                    waited.append(kind)
                src = {"x": T.xs[:], "w": T.ws[:], "p": col(T.pl, s)}[kind]
                dst = {"x": col(T.xl, s), "w": T.ws[:], "p": col(T.pl, s)}[kind]
                ids = [DstId(rid=topo.addr(d)[0], pnc=topo.addr(d)[1]) for d in to]
                trs.append(RemoteDMATransfer(dst_ids=ids, dma_engine_mask=_mk(eng), remote_sem=S[_semname(kind, s)],
                                             srcs=[src], dsts=[dst for _ in to], alu_op=0))
                sent[0] += len(eng)
            g.remote_dma_fused(trs, local_sem=S.snt)

    g.sync.dma_start(T.xs[:], T.x[:]).then_inc(S.ldx, 16)
    if pos == 0:
        g.scalar.dma_start(T.ws[:], T.w[:]).then_inc(S.ldw, 16)

    issue(calls[core][0])

    v = g.vector
    pe = g.tensor
    if leader:
        acc = [T.acc0[:, 0:H], T.acc1[:, 0:H]]
        own = [T.pp0[:, 0:H], T.pp1[:, 0:H]]
        v.memset(T.zi[:, 0:1], 1.0).then_inc(S.zi1, 1)
        v.memset(T.zi[:, 1:129], 0.0).then_inc(S.zi1, 1)
        v.memset(T.zero[:], 0.0).then_inc(S.zf, 1)
        g.scalar.wait_ge(S.zi1, 2)
        g.scalar.dma_start(T.idd[:], T.zi[:]).then_inc(S.id1, 16)
        g.scalar.wait_ge(S.id1, 16)
        g.scalar.dma_start(T.idn[:], T.idd[0:128, :]).then_inc(S.id2, 16)
        pe.wait_ge(S.id2, 16)
        pe.wait_ge(S.ldx, 16)
        for h in range(2):
            pe.matmul(acc[h], T.idn[:], half(T.xs, 0, h), start=True, stop=False)
        order = sorted([a for a in due if a.startswith("ax")], key=lambda a: eta[a])
        for nm in order:
            pe.wait_ge(S[nm], due[nm])
            for h in range(2):
                last = nm == order[-1]
                ins = pe.matmul(acc[h], T.idn[:], half(T.xl, int(nm[2:]), h), start=False, stop=last)
                if last:
                    ins.then_inc(S["sm%d" % h], 1)
        v.wait_ge(S.zf, 1)
        for h in range(2):
            v.wait_ge(S["sm%d" % h], 1)
            v.tensor_tensor(half(T.ts, 0, h), acc[h], T.zero[:], AluOpType.max).then_inc(S["tr%d" % h], 1)
        if pos == 0:
            pe.wait_ge(S.ldw, 16)
        else:
            pe.wait_ge(S.aw, due["aw"])
        for h in range(2):
            pe.wait_ge(S["tr%d" % h], 1)
            pe.matmul(own[h], T.ws[:], half(T.ts, 0, h), start=True, stop=True).then_inc(S["mm%d" % h], 1)
        for h in range(2):
            v.wait_ge(S["mm%d" % h], 1)
            v.tensor_copy(half(T.pl, gi, h), own[h]).then_inc(S.pr, 1)
        issue(calls[core][1])
        v.wait_ge(S.ap, due["ap"])
        for h in range(2):
            v.tensor_tensor(half(T.ys, 0, h), own[h], half(T.pl, 1 - gi, h), AluOpType.add).then_inc(S.yr, 1)
    else:
        v.wait_ge(S.ap, due["ap"])
        v.tensor_tensor(T.ys[:], col(T.pl, 0), col(T.pl, 1), AluOpType.add).then_inc(S.yr, 2)

    g.sync.wait_ge(S.yr, 2)
    g.sync.dma_start(T.y[:], T.ys[:]).then_inc(S.st, 16)
    g.wait_ge(S.snt, sent[0])
    g.wait_ge(S.st, 16)
